import numpy as np
import ml_dtypes


def mxq(x, axis, fmt="e4m3"):
    dtype, down = {"e4m3": (ml_dtypes.float8_e4m3fn, 7), "e5m2": (ml_dtypes.float8_e5m2, 14)}[fmt]
    v = np.moveaxis(np.asarray(x, np.float32).astype(ml_dtypes.bfloat16).astype(np.float64), axis, -1)
    blocks = v.reshape(v.shape[:-1] + (-1, 32))
    amax = np.abs(blocks).max(-1, keepdims=True)
    byte = np.maximum(np.where(amax > 0, np.frexp(amax)[1] - 1 + 127, 0) - down, 1)
    scale = np.exp2(byte - 127.0)
    codes = (blocks / scale).astype(np.float32).astype(dtype).astype(np.float64)
    return np.moveaxis((codes * scale).reshape(v.shape), -1, axis)


WIDE = False


def mx_kscale(k):
    if not WIDE:
        return np.ones(k)
    levels = np.array([10, -10, 5, -5, 0])
    if k % 512:
        return np.exp2(np.random.permutation(np.resize(levels, k // 32))).repeat(32)
    a = np.empty((k // 512, 16))
    for p in range(k // 512):
        a[p, :8] = np.random.permutation(np.resize(levels, 8))
        for g in range(8):
            far = levels[np.abs(levels - a[p, g]) >= 10]
            a[p, g + 8] = far[np.random.randint(len(far))]
    return np.exp2(a.ravel()).repeat(32)


def f64(x):
    return np.asarray(x).astype(np.float64)


def striped(idx):
    return np.tile(idx.reshape(-1, 16).T, (8, 1)).astype(np.uint16)


def unstriped(offs):
    return offs[:16].T.reshape(-1).astype(np.int64)

def planes(y):
    n, m = y.shape
    v = y.astype(np.float32).astype(ml_dtypes.bfloat16).astype(np.float64).reshape(n // 32, 32, m)
    top = np.abs(v).max(1)
    byte = np.clip(np.where(top > 0, np.frexp(top)[1] - 1 + 127 - 7, 1), 1, 254)
    codes = (v * np.exp2(127.0 - byte)[:, None, :]).reshape(n, m).astype(np.float32).astype(ml_dtypes.float8_e4m3fn).view(np.uint8)
    words = codes.reshape(n // 512, 128, 4, m).transpose(0, 1, 3, 2)
    return np.ascontiguousarray(words), np.ascontiguousarray(byte.astype(np.uint8).reshape(n // 512, 16, m))


K, T, S, N, U = 512, 2048, 512, 512, 1024


def setup_inputs():
    n = np.random.standard_normal
    s = mx_kscale(K)[:, None]
    return {
        "xT": (n((K, T)) * s).astype(np.float32),
        "w1": (n((K, N)) / np.sqrt(K) / s).astype(np.float32),
        "gamma": np.random.uniform(0.5, 1.5, (N, U)).astype(np.float32),
        "beta": (0.5 * n((N, U))).astype(np.float32),
        "offs": striped(np.random.permutation(T)[:S]),
        "cls": striped(np.random.randint(0, U, S)),
    }


def reference(xT, w1, gamma, beta, offs, cls):
    xq = mxq(f64(xT)[:, unstriped(offs)], 0, "e4m3")
    y = mxq(f64(w1), 0, "e4m3").T @ xq
    g = f64(gamma)[:, unstriped(cls)]
    s = f64(beta)[:, unstriped(cls)]
    out_0 = y * g + s
    return (out_0,) + planes(out_0)

@@ -1,0 +1,122 @@
+from contextlib import ExitStack
+
+import concourse.mybir as mybir
+
+K, T, S, N, U = 512, 2048, 512, 512, 1024
+FLOPS = 2 * K * N * S
+
+F32 = mybir.dt.float32
+BF16 = mybir.dt.bfloat16
+I32 = mybir.dt.int32
+U32 = mybir.dt.uint32
+U16 = mybir.dt.uint16
+U8 = mybir.dt.uint8
+FP8X4 = mybir.dt.float8_e4m3fn_x4
+MULT = mybir.AluOpType.mult
+ADD = mybir.AluOpType.add
+
+P = 128
+PACK = 4
+HALF = S // 2
+
+
+def tile_picked_cbn_none_lo_kernel(tc, xT, w1, gamma, beta, offs, cls, out_0, out_1, out_2):
+    nc = tc.nc
+    with ExitStack() as ctx:
+        keep = ctx.enter_context(tc.tile_pool(name="keep", bufs=1))
+        psum = ctx.enter_context(tc.psum_pool(name="psum", bufs=1))
+
+        offs_sb = keep.tile([P, S // 16], U16, name="offs_sb")
+        cls_sb = keep.tile([P, S // 16], U16, name="cls_sb")
+        x_rows = xT.rearrange("(p j) c -> p j c", j=PACK)
+        w_rows = w1.rearrange("(p j) c -> p j c", j=PACK)
+        g_rows = gamma.rearrange("(p t) c -> p t c", t=PACK)
+        b_rows = beta.rearrange("(p t) c -> p t c", t=PACK)
+        o_rows = out_0.rearrange("(p t) c -> p t c", t=PACK)
+
+        x_sb = [keep.tile([P, T], F32, name=f"x{j}") for j in range(PACK)]
+        w_sb = [keep.tile([P, 2, N], F32, name=f"w{h}") for h in range(2)]
+        g_sb = [keep.tile([P, U], F32, name=f"g{t}") for t in range(PACK)]
+        b_sb = [keep.tile([P, U], F32, name=f"b{t}") for t in range(PACK)]
+
+        nc.sync.dma_start(x_sb[0][:], x_rows[:, 0, :])
+        nc.sync.dma_start(offs_sb[:], offs)
+        for j in range(1, PACK):
+            nc.sync.dma_start(x_sb[j][:], x_rows[:, j, :])
+        for h in range(2):
+            nc.sync.dma_start(w_sb[h][:], w_rows[:, 2 * h : 2 * h + 2, :])
+        nc.sync.dma_start(cls_sb[:], cls)
+        for t in range(PACK):
+            nc.sync.dma_start(g_sb[t][:], g_rows[:, t, :])
+            nc.sync.dma_start(b_sb[t][:], b_rows[:, t, :])
+
+        x_bf = keep.tile([P, S, PACK], BF16, name="x_bf", align_bytes=64)
+        for j in range(PACK):
+            nc.vector.tensor_copy(x_bf[:, :, j], x_sb[j][:].indirect(offs_sb[:]))
+        x_codes = keep.tile([P, S], U32, name="x_codes", align_bytes=64)
+        x_scales = keep.tile([P, S], U8, name="x_scales", align_bytes=64)
+        nc.vector.quantize_mx(out=x_codes[:].bitcast(FP8X4), scales=x_scales[:], in_=x_bf[:].rearrange("p s j -> p (s j)"))
+
+        w_bf = keep.tile([P, PACK, P, PACK], BF16, name="w_bf", align_bytes=64)
+        w_walk = w_bf[:].rearrange("p t m j -> p m t j")
+        nc.scalar.copy(w_walk[:, :, :, 0:2], w_sb[0][:].rearrange("p j (m t) -> p m t j", t=PACK))
+        nc.vector.tensor_copy(w_walk[:, :, :, 2:4], w_sb[1][:].rearrange("p j (m t) -> p m t j", t=PACK))
+        w_codes = keep.tile([P, N], U32, name="w_codes", align_bytes=64)
+        w_scales = keep.tile([P, N], U8, name="w_scales", align_bytes=64)
+        nc.vector.quantize_mx(out=w_codes[:].bitcast(FP8X4), scales=w_scales[:], in_=w_bf[:].rearrange("p t m j -> p (t m j)"))
+
+        res = [keep.tile([P, 2, S], F32, name=f"res{u}") for u in range(2)]
+        o_bf = [keep.tile([P, HALF, PACK], BF16, name=f"o_bf{h}", align_bytes=64) for h in range(2)]
+        o_codes = keep.tile([P, S], U32, name="o_codes", align_bytes=64)
+        o_scales = keep.tile([P, S], U8, name="o_scales", align_bytes=64)
+
+        for t in range(PACK):
+            acc = psum.tile([P, S], F32, name=f"acc{t}")
+            cols = slice(t * P, (t + 1) * P)
+            nc.tensor.matmul_mx(
+                out=acc[:],
+                lhsT=w_codes[:, cols].bitcast(FP8X4),
+                lhsT_scale=w_scales[:, cols],
+                rhs=x_codes[:].bitcast(FP8X4),
+                rhs_scale=x_scales[:],
+                start=True,
+                stop=True,
+            )
+            scaled = keep.tile([P, S], F32, name=f"scaled{t}")
+            if t == 0:
+                g_picked = keep.tile([P, S], F32, name="g_picked")
+                nc.vector.tensor_copy(g_picked[:], g_sb[t][:].indirect(cls_sb[:]))
+                nc.vector.tensor_tensor(scaled[:], acc[:], g_picked[:], MULT)
+            else:
+                y_sb = keep.tile([P, S], F32, name=f"y{t}")
+                nc.scalar.copy(y_sb[:], acc[:])
+                nc.vector.tensor_tensor(scaled[:], g_sb[t][:].indirect(cls_sb[:]), y_sb[:], MULT)
+            row = res[t // 2][:, t % 2, :]
+            if t < PACK - 1:
+                nc.vector.tensor_tensor(row, b_sb[t][:].indirect(cls_sb[:]), scaled[:], ADD)
+                nc.sync.dma_start(o_rows[:, t, :], row)
+            else:
+                for h in range(2):
+                    part = slice(h * HALF, (h + 1) * HALF)
+                    entries = cls_sb[:, h * HALF // 16 : (h + 1) * HALF // 16]
+                    nc.vector.tensor_tensor(row[:, part], b_sb[t][:].indirect(entries), scaled[:, part], ADD)
+                    nc.sync.dma_start(o_rows[:, t, part], row[:, part])
+            if t == 1:
+                for h in range(2):
+                    part = slice(h * HALF, (h + 1) * HALF)
+                    nc.scalar.copy(o_bf[h][:, :, 0:2], res[0][:, :, part].rearrange("p t s -> p s t"))
+
+        words = out_1.rearrange("z p s r -> p (z s r)").bitcast(I32)
+        for h in range(2):
+            part = slice(h * HALF, (h + 1) * HALF)
+            pair = res[1][:, :, part].rearrange("p t s -> p s t")
+            if h == 0:
+                nc.scalar.copy(o_bf[h][:, :, 2:4], pair)
+            else:
+                nc.vector.tensor_copy(o_bf[h][:, :, 2:4], pair)
+            nc.vector.quantize_mx(out=o_codes[:, part].bitcast(FP8X4), scales=o_scales[:, part], in_=o_bf[h][:].rearrange("p s t -> p (s t)"))
+            nc.sync.dma_start(words[:, part], o_codes[:, part].bitcast(I32))
+        scale_rows = out_2.rearrange("z q s -> (z q) s").bitcast(I32)
+        for q in range(4):
+            queue = nc.scalar if q % 2 == 0 else nc.sync
+            queue.dma_start(scale_rows[4 * q : 4 * q + 4, :], o_scales[32 * q : 32 * q + 4, :].bitcast(I32))

@@ -35,7 +35,7 @@ def tile_picked_cbn_none_lo_kernel(tc, xT, w1, gamma, beta, offs, cls, out_0, ou
         o_rows = out_0.rearrange("(p t) c -> p t c", t=PACK)
 
         x_sb = [keep.tile([P, T], F32, name=f"x{j}") for j in range(PACK)]
-        w_sb = [keep.tile([P, 2, N], F32, name=f"w{h}") for h in range(2)]
+        w_sb = keep.tile([P, PACK, N], F32, name="w_sb")
         g_sb = [keep.tile([P, U], F32, name=f"g{t}") for t in range(PACK)]
         b_sb = [keep.tile([P, U], F32, name=f"b{t}") for t in range(PACK)]
 
@@ -43,68 +43,81 @@ def tile_picked_cbn_none_lo_kernel(tc, xT, w1, gamma, beta, offs, cls, out_0, ou
         nc.sync.dma_start(offs_sb[:], offs)
         for j in range(1, PACK):
             nc.sync.dma_start(x_sb[j][:], x_rows[:, j, :])
-        for h in range(2):
-            nc.sync.dma_start(w_sb[h][:], w_rows[:, 2 * h : 2 * h + 2, :])
+        nc.sync.dma_start(w_sb[:], w_rows)
         nc.sync.dma_start(cls_sb[:], cls)
-        for t in range(PACK):
-            nc.sync.dma_start(g_sb[t][:], g_rows[:, t, :])
-            nc.sync.dma_start(b_sb[t][:], b_rows[:, t, :])
+        for t in range(PACK + 1):
+            if t < PACK:
+                nc.sync.dma_start(g_sb[t][:], g_rows[:, t, :])
+            if t > 0:
+                nc.sync.dma_start(b_sb[t - 1][:], b_rows[:, t - 1, :])
 
-        x_bf = keep.tile([P, S, PACK], BF16, name="x_bf", align_bytes=64)
+        halves = [slice(h * HALF, (h + 1) * HALF) for h in range(2)]
+        list_halves = [slice(h * HALF // 16, (h + 1) * HALF // 16) for h in range(2)]
+        x_bf = [keep.tile([P, HALF, PACK], BF16, name=f"x_bf{h}", align_bytes=64) for h in range(2)]
         for j in range(PACK):
-            nc.vector.tensor_copy(x_bf[:, :, j], x_sb[j][:].indirect(offs_sb[:]))
+            for h in range(2):
+                nc.vector.tensor_copy(x_bf[h][:, :, j], x_sb[j][:].indirect(offs_sb[:, list_halves[h]]))
         x_codes = keep.tile([P, S], U32, name="x_codes", align_bytes=64)
         x_scales = keep.tile([P, S], U8, name="x_scales", align_bytes=64)
-        nc.vector.quantize_mx(out=x_codes[:].bitcast(FP8X4), scales=x_scales[:], in_=x_bf[:].rearrange("p s j -> p (s j)"))
+        for h in range(2):
+            nc.vector.quantize_mx(out=x_codes[:, halves[h]].bitcast(FP8X4), scales=x_scales[:, halves[h]], in_=x_bf[h][:].rearrange("p s j -> p (s j)"))
 
-        w_bf = keep.tile([P, PACK, P, PACK], BF16, name="w_bf", align_bytes=64)
-        w_walk = w_bf[:].rearrange("p t m j -> p m t j")
-        nc.scalar.copy(w_walk[:, :, :, 0:2], w_sb[0][:].rearrange("p j (m t) -> p m t j", t=PACK))
-        nc.vector.tensor_copy(w_walk[:, :, :, 2:4], w_sb[1][:].rearrange("p j (m t) -> p m t j", t=PACK))
-        w_codes = keep.tile([P, N], U32, name="w_codes", align_bytes=64)
-        w_scales = keep.tile([P, N], U8, name="w_scales", align_bytes=64)
-        nc.vector.quantize_mx(out=w_codes[:].bitcast(FP8X4), scales=w_scales[:], in_=w_bf[:].rearrange("p t m j -> p (t m j)"))
+        w_walk = w_sb[:].rearrange("p j (m t) -> p m t j", t=PACK)
+        w_codes, w_scales = [], []
+        for u in range(2):
+            w_bf = keep.tile([P, 2, P, PACK], BF16, name=f"w_bf{u}", align_bytes=64)
+            copy = nc.vector.tensor_copy if u == 0 else nc.scalar.copy
+            copy(w_bf[:].rearrange("p t m j -> p m t j"), w_walk[:, :, 2 * u : 2 * u + 2, :])
+            w_codes.append(keep.tile([P, 2 * P], U32, name=f"w_codes{u}", align_bytes=64))
+            w_scales.append(keep.tile([P, 2 * P], U8, name=f"w_scales{u}", align_bytes=64))
+            nc.vector.quantize_mx(out=w_codes[u][:].bitcast(FP8X4), scales=w_scales[u][:], in_=w_bf[:].rearrange("p t m j -> p (t m j)"))
 
         res = [keep.tile([P, 2, S], F32, name=f"res{u}") for u in range(2)]
         o_bf = [keep.tile([P, HALF, PACK], BF16, name=f"o_bf{h}", align_bytes=64) for h in range(2)]
         o_codes = keep.tile([P, S], U32, name="o_codes", align_bytes=64)
         o_scales = keep.tile([P, S], U8, name="o_scales", align_bytes=64)
 
-        for t in range(PACK):
+        scaled = [keep.tile([P, S], F32, name=f"scaled{t}") for t in range(PACK)]
+
+        def scale(t):
             acc = psum.tile([P, S], F32, name=f"acc{t}")
-            cols = slice(t * P, (t + 1) * P)
+            cols = slice((t % 2) * P, (t % 2 + 1) * P)
             nc.tensor.matmul_mx(
                 out=acc[:],
-                lhsT=w_codes[:, cols].bitcast(FP8X4),
-                lhsT_scale=w_scales[:, cols],
+                lhsT=w_codes[t // 2][:, cols].bitcast(FP8X4),
+                lhsT_scale=w_scales[t // 2][:, cols],
                 rhs=x_codes[:].bitcast(FP8X4),
                 rhs_scale=x_scales[:],
                 start=True,
                 stop=True,
             )
-            scaled = keep.tile([P, S], F32, name=f"scaled{t}")
             if t == 0:
                 g_picked = keep.tile([P, S], F32, name="g_picked")
                 nc.vector.tensor_copy(g_picked[:], g_sb[t][:].indirect(cls_sb[:]))
-                nc.vector.tensor_tensor(scaled[:], acc[:], g_picked[:], MULT)
+                nc.vector.tensor_tensor(scaled[t][:], acc[:], g_picked[:], MULT)
             else:
                 y_sb = keep.tile([P, S], F32, name=f"y{t}")
                 nc.scalar.copy(y_sb[:], acc[:])
-                nc.vector.tensor_tensor(scaled[:], g_sb[t][:].indirect(cls_sb[:]), y_sb[:], MULT)
+                nc.vector.tensor_tensor(scaled[t][:], g_sb[t][:].indirect(cls_sb[:]), y_sb[:], MULT)
+
+        def shift(t):
             row = res[t // 2][:, t % 2, :]
             if t < PACK - 1:
-                nc.vector.tensor_tensor(row, b_sb[t][:].indirect(cls_sb[:]), scaled[:], ADD)
+                nc.vector.tensor_tensor(row, b_sb[t][:].indirect(cls_sb[:]), scaled[t][:], ADD)
                 nc.sync.dma_start(o_rows[:, t, :], row)
             else:
                 for h in range(2):
-                    part = slice(h * HALF, (h + 1) * HALF)
-                    entries = cls_sb[:, h * HALF // 16 : (h + 1) * HALF // 16]
-                    nc.vector.tensor_tensor(row[:, part], b_sb[t][:].indirect(entries), scaled[:, part], ADD)
-                    nc.sync.dma_start(o_rows[:, t, part], row[:, part])
+                    nc.vector.tensor_tensor(row[:, halves[h]], b_sb[t][:].indirect(cls_sb[:, list_halves[h]]), scaled[t][:, halves[h]], ADD)
+                    nc.sync.dma_start(o_rows[:, t, halves[h]], row[:, halves[h]])
             if t == 1:
                 for h in range(2):
-                    part = slice(h * HALF, (h + 1) * HALF)
-                    nc.scalar.copy(o_bf[h][:, :, 0:2], res[0][:, :, part].rearrange("p t s -> p s t"))
+                    nc.scalar.copy(o_bf[h][:, :, 0:2], res[0][:, :, halves[h]].rearrange("p t s -> p s t"))
+
+        for t in range(PACK + 1):
+            if t < PACK:
+                scale(t)
+            if t > 0:
+                shift(t - 1)
 
         words = out_1.rearrange("z p s r -> p (z s r)").bitcast(I32)
         for h in range(2):

@@ -1,6 +1,7 @@
 from contextlib import ExitStack
 
 import concourse.mybir as mybir
+from concourse.masks import make_identity
 
 K, T, S, N, U = 512, 2048, 512, 512, 1024
 FLOPS = 2 * K * N * S
@@ -45,11 +46,15 @@ def tile_picked_cbn_none_lo_kernel(tc, xT, w1, gamma, beta, offs, cls, out_0, ou
             nc.sync.dma_start(x_sb[j][:], x_rows[:, j, :])
         nc.sync.dma_start(w_sb[:], w_rows)
         nc.sync.dma_start(cls_sb[:], cls)
-        for t in range(PACK + 1):
+        nc.sync.dma_start(b_sb[0][:], b_rows[:, 0, :])
+        nc.sync.dma_start(g_sb[0][:], g_rows[:, 0, :])
+        for t in range(1, PACK + 1):
             if t < PACK:
                 nc.sync.dma_start(g_sb[t][:], g_rows[:, t, :])
-            if t > 0:
+            if t > 1:
                 nc.sync.dma_start(b_sb[t - 1][:], b_rows[:, t - 1, :])
+        ident = keep.tile([P, P], F32, name="ident")
+        make_identity(nc, ident[:])
 
         halves = [slice(h * HALF, (h + 1) * HALF) for h in range(2)]
         list_halves = [slice(h * HALF // 16, (h + 1) * HALF // 16) for h in range(2)]
@@ -79,6 +84,9 @@ def tile_picked_cbn_none_lo_kernel(tc, xT, w1, gamma, beta, offs, cls, out_0, ou
 
         scaled = [keep.tile([P, S], F32, name=f"scaled{t}") for t in range(PACK)]
 
+        b_picked = keep.tile([P, S], F32, name="b_picked")
+        nc.vector.tensor_copy(b_picked[:], b_sb[0][:].indirect(cls_sb[:]))
+
         def scale(t):
             acc = psum.tile([P, S], F32, name=f"acc{t}")
             cols = slice((t % 2) * P, (t % 2 + 1) * P)
@@ -91,18 +99,27 @@ def tile_picked_cbn_none_lo_kernel(tc, xT, w1, gamma, beta, offs, cls, out_0, ou
                 start=True,
                 stop=True,
             )
-            if t == 0:
-                g_picked = keep.tile([P, S], F32, name="g_picked")
-                nc.vector.tensor_copy(g_picked[:], g_sb[t][:].indirect(cls_sb[:]))
-                nc.vector.tensor_tensor(scaled[t][:], acc[:], g_picked[:], MULT)
-            else:
-                y_sb = keep.tile([P, S], F32, name=f"y{t}")
-                nc.scalar.copy(y_sb[:], acc[:])
-                nc.vector.tensor_tensor(scaled[t][:], g_sb[t][:].indirect(cls_sb[:]), y_sb[:], MULT)
+            y_sb = keep.tile([P, S], F32, name=f"y{t}")
+            nc.scalar.copy(y_sb[:], acc[:])
+            nc.vector.tensor_tensor(scaled[t][:], g_sb[t][:].indirect(cls_sb[:]), y_sb[:], MULT)
 
         def shift(t):
             row = res[t // 2][:, t % 2, :]
-            if t < PACK - 1:
+            if t == 0:
+                turned = psum.tile([P, S], F32, name="turned")
+                for c in range(S // P):
+                    cols = slice(c * P, (c + 1) * P)
+                    nc.tensor.matmul(turned[:, cols], b_picked[:, cols], ident[:], start=True, stop=False, is_transpose=True)
+                    nc.tensor.matmul(turned[:, cols], scaled[t][:, cols], ident[:], start=False, stop=True, is_transpose=True)
+                turned_sb = keep.tile([P, S], F32, name="turned_sb")
+                nc.scalar.copy(turned_sb[:], turned[:])
+                back = psum.tile([P, S], F32, name="back")
+                for c in range(S // P):
+                    cols = slice(c * P, (c + 1) * P)
+                    nc.tensor.transpose(back[:, cols], turned_sb[:, cols], ident[:])
+                nc.scalar.copy(row, back[:])
+                nc.sync.dma_start(o_rows[:, t, :], row)
+            elif t < PACK - 1:
                 nc.vector.tensor_tensor(row, b_sb[t][:].indirect(cls_sb[:]), scaled[t][:], ADD)
                 nc.sync.dma_start(o_rows[:, t, :], row)
             else:

@@ -19,6 +19,7 @@ ADD = mybir.AluOpType.add
 P = 128
 PACK = 4
 HALF = S // 2
+TAIL = ((0, HALF), (HALF, HALF + HALF // 2), (HALF + HALF // 2, S))
 
 
 def tile_picked_cbn_none_lo_kernel(tc, xT, w1, gamma, beta, offs, cls, out_0, out_1, out_2):
@@ -87,21 +88,21 @@ def tile_picked_cbn_none_lo_kernel(tc, xT, w1, gamma, beta, offs, cls, out_0, ou
         b_picked = keep.tile([P, S], F32, name="b_picked")
         nc.vector.tensor_copy(b_picked[:], b_sb[0][:].indirect(cls_sb[:]))
 
-        def scale(t):
-            acc = psum.tile([P, S], F32, name=f"acc{t}")
+        def scale(t, lo, hi):
+            acc = psum.tile([P, hi - lo], F32, name=f"acc{t}_{lo}")
             cols = slice((t % 2) * P, (t % 2 + 1) * P)
             nc.tensor.matmul_mx(
                 out=acc[:],
                 lhsT=w_codes[t // 2][:, cols].bitcast(FP8X4),
                 lhsT_scale=w_scales[t // 2][:, cols],
-                rhs=x_codes[:].bitcast(FP8X4),
-                rhs_scale=x_scales[:],
+                rhs=x_codes[:, lo:hi].bitcast(FP8X4),
+                rhs_scale=x_scales[:, lo:hi],
                 start=True,
                 stop=True,
             )
-            y_sb = keep.tile([P, S], F32, name=f"y{t}")
+            y_sb = keep.tile([P, hi - lo], F32, name=f"y{t}_{lo}")
             nc.scalar.copy(y_sb[:], acc[:])
-            nc.vector.tensor_tensor(scaled[t][:], g_sb[t][:].indirect(cls_sb[:]), y_sb[:], MULT)
+            nc.vector.tensor_tensor(scaled[t][:, lo:hi], g_sb[t][:].indirect(cls_sb[:, lo // 16 : hi // 16]), y_sb[:], MULT)
 
         def shift(t):
             row = res[t // 2][:, t % 2, :]
@@ -123,29 +124,33 @@ def tile_picked_cbn_none_lo_kernel(tc, xT, w1, gamma, beta, offs, cls, out_0, ou
                 nc.vector.tensor_tensor(row, b_sb[t][:].indirect(cls_sb[:]), scaled[t][:], ADD)
                 nc.sync.dma_start(o_rows[:, t, :], row)
             else:
-                for h in range(2):
-                    nc.vector.tensor_tensor(row[:, halves[h]], b_sb[t][:].indirect(cls_sb[:, list_halves[h]]), scaled[t][:, halves[h]], ADD)
-                    nc.sync.dma_start(o_rows[:, t, halves[h]], row[:, halves[h]])
+                for lo, hi in TAIL:
+                    nc.vector.tensor_tensor(row[:, lo:hi], b_sb[t][:].indirect(cls_sb[:, lo // 16 : hi // 16]), scaled[t][:, lo:hi], ADD)
+                    if hi % HALF == 0:
+                        nc.sync.dma_start(o_rows[:, t, hi - HALF : hi], row[:, hi - HALF : hi])
             if t == 1:
                 for h in range(2):
                     nc.scalar.copy(o_bf[h][:, :, 0:2], res[0][:, :, halves[h]].rearrange("p t s -> p s t"))
 
         for t in range(PACK + 1):
-            if t < PACK:
-                scale(t)
+            if t == 0:
+                for h in range(2):
+                    scale(t, h * HALF, (h + 1) * HALF)
+            elif t < PACK:
+                scale(t, 0, S)
             if t > 0:
                 shift(t - 1)
 
         words = out_1.rearrange("z p s r -> p (z s r)").bitcast(I32)
-        for h in range(2):
-            part = slice(h * HALF, (h + 1) * HALF)
-            pair = res[1][:, :, part].rearrange("p t s -> p s t")
-            if h == 0:
-                nc.scalar.copy(o_bf[h][:, :, 2:4], pair)
-            else:
-                nc.vector.tensor_copy(o_bf[h][:, :, 2:4], pair)
-            nc.vector.quantize_mx(out=o_codes[:, part].bitcast(FP8X4), scales=o_scales[:, part], in_=o_bf[h][:].rearrange("p s t -> p (s t)"))
-            nc.sync.dma_start(words[:, part], o_codes[:, part].bitcast(I32))
+        for lo, hi in TAIL:
+            h = lo // HALF
+            copy = nc.scalar.copy if h == 0 else nc.vector.tensor_copy
+            copy(o_bf[h][:, lo - h * HALF : hi - h * HALF, 2:4], res[1][:, :, lo:hi].rearrange("p t s -> p s t"))
+        for lo, hi in TAIL[1:] + TAIL[:1]:
+            h = lo // HALF
+            nc.vector.quantize_mx(out=o_codes[:, lo:hi].bitcast(FP8X4), scales=o_scales[:, lo:hi], in_=o_bf[h][:, lo - h * HALF : hi - h * HALF, :].rearrange("p s t -> p (s t)"))
+            if hi % HALF == 0:
+                nc.sync.dma_start(words[:, hi - HALF : hi], o_codes[:, hi - HALF : hi].bitcast(I32))
         scale_rows = out_2.rearrange("z q s -> (z q) s").bitcast(I32)
         for q in range(4):
             queue = nc.scalar if q % 2 == 0 else nc.sync

@@ -36,17 +36,18 @@ def tile_picked_cbn_none_lo_kernel(tc, xT, w1, gamma, beta, offs, cls, out_0, ou
         b_rows = beta.rearrange("(p t) c -> p t c", t=PACK)
         o_rows = out_0.rearrange("(p t) c -> p t c", t=PACK)
 
-        x_sb = [keep.tile([P, T], F32, name=f"x{j}") for j in range(PACK)]
+        x_first = keep.tile([P, 2 * T], F32, name="x_first")
+        x_late = [keep.tile([P, T], F32, name=f"x{j}") for j in range(2, PACK)]
         w_sb = keep.tile([P, PACK, N], F32, name="w_sb")
         g_sb = [keep.tile([P, U], F32, name=f"g{t}") for t in range(PACK)]
         b_sb = [keep.tile([P, U], F32, name=f"b{t}") for t in range(PACK)]
 
-        nc.sync.dma_start(x_sb[0][:], x_rows[:, 0, :])
+        nc.sync.dma_start(x_first[:], x_rows[:, 0:2, :].rearrange("p j c -> p (j c)"))
         nc.sync.dma_start(offs_sb[:], offs)
-        for j in range(1, PACK):
-            nc.sync.dma_start(x_sb[j][:], x_rows[:, j, :])
-        nc.sync.dma_start(w_sb[:], w_rows)
         nc.sync.dma_start(cls_sb[:], cls)
+        for j in range(2, PACK):
+            nc.sync.dma_start(x_late[j - 2][:], x_rows[:, j, :])
+        nc.sync.dma_start(w_sb[:], w_rows)
         nc.sync.dma_start(b_sb[0][:], b_rows[:, 0, :])
         nc.sync.dma_start(g_sb[0][:], g_rows[:, 0, :])
         for t in range(1, PACK + 1):
@@ -60,20 +61,28 @@ def tile_picked_cbn_none_lo_kernel(tc, xT, w1, gamma, beta, offs, cls, out_0, ou
         halves = [slice(h * HALF, (h + 1) * HALF) for h in range(2)]
         list_halves = [slice(h * HALF // 16, (h + 1) * HALF // 16) for h in range(2)]
         x_bf = [keep.tile([P, HALF, PACK], BF16, name=f"x_bf{h}", align_bytes=64) for h in range(2)]
-        for j in range(PACK):
+        x_picked = keep.tile([P, 2, S], F32, name="x_picked")
+        for j in range(2):
+            nc.vector.tensor_copy(x_picked[:, j, :], x_first[:, j * T : (j + 1) * T].indirect(offs_sb[:]))
+        for h in range(2):
+            nc.scalar.copy(x_bf[h][:, :, 0:2], x_picked[:, :, halves[h]].rearrange("p j s -> p s j"))
+        for j in range(2, PACK):
             for h in range(2):
-                nc.vector.tensor_copy(x_bf[h][:, :, j], x_sb[j][:].indirect(offs_sb[:, list_halves[h]]))
+                nc.vector.tensor_copy(x_bf[h][:, :, j], x_late[j - 2][:].indirect(offs_sb[:, list_halves[h]]))
         x_codes = keep.tile([P, S], U32, name="x_codes", align_bytes=64)
         x_scales = keep.tile([P, S], U8, name="x_scales", align_bytes=64)
         for h in range(2):
             nc.vector.quantize_mx(out=x_codes[:, halves[h]].bitcast(FP8X4), scales=x_scales[:, halves[h]], in_=x_bf[h][:].rearrange("p s j -> p (s j)"))
 
         w_walk = w_sb[:].rearrange("p j (m t) -> p m t j", t=PACK)
+        b_picked = keep.tile([P, S], F32, name="b_picked")
         w_codes, w_scales = [], []
         for u in range(2):
             w_bf = keep.tile([P, 2, P, PACK], BF16, name=f"w_bf{u}", align_bytes=64)
             copy = nc.vector.tensor_copy if u == 0 else nc.scalar.copy
             copy(w_bf[:].rearrange("p t m j -> p m t j"), w_walk[:, :, 2 * u : 2 * u + 2, :])
+            if u == 1:
+                nc.vector.tensor_copy(b_picked[:], b_sb[0][:].indirect(cls_sb[:]))
             w_codes.append(keep.tile([P, 2 * P], U32, name=f"w_codes{u}", align_bytes=64))
             w_scales.append(keep.tile([P, 2 * P], U8, name=f"w_scales{u}", align_bytes=64))
             nc.vector.quantize_mx(out=w_codes[u][:].bitcast(FP8X4), scales=w_scales[u][:], in_=w_bf[:].rearrange("p t m j -> p (t m j)"))
@@ -85,8 +94,6 @@ def tile_picked_cbn_none_lo_kernel(tc, xT, w1, gamma, beta, offs, cls, out_0, ou
 
         scaled = [keep.tile([P, S], F32, name=f"scaled{t}") for t in range(PACK)]
 
-        b_picked = keep.tile([P, S], F32, name="b_picked")
-        nc.vector.tensor_copy(b_picked[:], b_sb[0][:].indirect(cls_sb[:]))
 
         def scale(t, lo, hi):
             acc = psum.tile([P, hi - lo], F32, name=f"acc{t}_{lo}")
@@ -126,8 +133,7 @@ def tile_picked_cbn_none_lo_kernel(tc, xT, w1, gamma, beta, offs, cls, out_0, ou
             else:
                 for lo, hi in TAIL:
                     nc.vector.tensor_tensor(row[:, lo:hi], b_sb[t][:].indirect(cls_sb[:, lo // 16 : hi // 16]), scaled[t][:, lo:hi], ADD)
-                    if hi % HALF == 0:
-                        nc.sync.dma_start(o_rows[:, t, hi - HALF : hi], row[:, hi - HALF : hi])
+                nc.sync.dma_start(o_rows[:, t, :], row)
             if t == 1:
                 for h in range(2):
                     nc.scalar.copy(o_bf[h][:, :, 0:2], res[0][:, :, halves[h]].rearrange("p t s -> p s t"))

@@ -19,7 +19,8 @@ ADD = mybir.AluOpType.add
 P = 128
 PACK = 4
 HALF = S // 2
-TAIL = ((0, HALF), (HALF, HALF + HALF // 2), (HALF + HALF // 2, S))
+QUARTER = S // 4
+TAIL = tuple((q * QUARTER, (q + 1) * QUARTER) for q in (0, 2, 1, 3))
 
 
 def tile_picked_cbn_none_lo_kernel(tc, xT, w1, gamma, beta, offs, cls, out_0, out_1, out_2):
@@ -150,9 +151,9 @@ def tile_picked_cbn_none_lo_kernel(tc, xT, w1, gamma, beta, offs, cls, out_0, ou
         words = out_1.rearrange("z p s r -> p (z s r)").bitcast(I32)
         for lo, hi in TAIL:
             h = lo // HALF
-            copy = nc.scalar.copy if h == 0 else nc.vector.tensor_copy
+            copy = nc.vector.tensor_copy if lo == QUARTER else nc.scalar.copy
             copy(o_bf[h][:, lo - h * HALF : hi - h * HALF, 2:4], res[1][:, :, lo:hi].rearrange("p t s -> p s t"))
-        for lo, hi in TAIL[1:] + TAIL[:1]:
+        for lo, hi in TAIL[0::2] + TAIL[1::2]:
             h = lo // HALF
             nc.vector.quantize_mx(out=o_codes[:, lo:hi].bitcast(FP8X4), scales=o_scales[:, lo:hi], in_=o_bf[h][:, lo - h * HALF : hi - h * HALF, :].rearrange("p s t -> p (s t)"))
             if hi % HALF == 0:

@@ -20,6 +20,7 @@ P = 128
 PACK = 4
 HALF = S // 2
 QUARTER = S // 4
+W_SHARE = 88
 TAIL = tuple((q * QUARTER, (q + 1) * QUARTER) for q in (0, 2, 1, 3))
 
 
@@ -80,8 +81,12 @@ def tile_picked_cbn_none_lo_kernel(tc, xT, w1, gamma, beta, offs, cls, out_0, ou
         w_codes, w_scales = [], []
         for u in range(2):
             w_bf = keep.tile([P, 2, P, PACK], BF16, name=f"w_bf{u}", align_bytes=64)
-            copy = nc.vector.tensor_copy if u == 0 else nc.scalar.copy
-            copy(w_bf[:].rearrange("p t m j -> p m t j"), w_walk[:, :, 2 * u : 2 * u + 2, :])
+            w_dealt = w_bf[:].rearrange("p t m j -> p m t j")
+            if u == 0:
+                nc.vector.tensor_copy(w_dealt[:, :W_SHARE], w_walk[:, :W_SHARE, 0:2, :])
+                nc.scalar.copy(w_dealt[:, W_SHARE:], w_walk[:, W_SHARE:, 0:2, :])
+            else:
+                nc.scalar.copy(w_dealt, w_walk[:, :, 2:4, :])
             if u == 1:
                 nc.vector.tensor_copy(b_picked[:], b_sb[0][:].indirect(cls_sb[:]))
             w_codes.append(keep.tile([P, 2 * P], U32, name=f"w_codes{u}", align_bytes=64))

@@ -46,9 +46,9 @@ def tile_picked_cbn_none_lo_kernel(tc, xT, w1, gamma, beta, offs, cls, out_0, ou
 
         nc.sync.dma_start(x_first[:], x_rows[:, 0:2, :].rearrange("p j c -> p (j c)"))
         nc.sync.dma_start(offs_sb[:], offs)
-        nc.sync.dma_start(cls_sb[:], cls)
         for j in range(2, PACK):
             nc.sync.dma_start(x_late[j - 2][:], x_rows[:, j, :])
+        nc.sync.dma_start(cls_sb[:], cls)
         nc.sync.dma_start(w_sb[:], w_rows)
         nc.sync.dma_start(b_sb[0][:], b_rows[:, 0, :])
         nc.sync.dma_start(g_sb[0][:], g_rows[:, 0, :])

@@ -76,17 +76,17 @@ def tile_picked_cbn_none_lo_kernel(tc, xT, w1, gamma, beta, offs, cls, out_0, ou
         for h in range(2):
             nc.vector.quantize_mx(out=x_codes[:, halves[h]].bitcast(FP8X4), scales=x_scales[:, halves[h]], in_=x_bf[h][:].rearrange("p s j -> p (s j)"))
 
-        w_walk = w_sb[:].rearrange("p j (m t) -> p m t j", t=PACK)
+        w_walk = w_sb[:].rearrange("p j (m t) -> p m j t", t=PACK)
         b_picked = keep.tile([P, S], F32, name="b_picked")
         w_codes, w_scales = [], []
         for u in range(2):
             w_bf = keep.tile([P, 2, P, PACK], BF16, name=f"w_bf{u}", align_bytes=64)
-            w_dealt = w_bf[:].rearrange("p t m j -> p m t j")
+            w_dealt = w_bf[:].rearrange("p t m j -> p m j t")
             if u == 0:
-                nc.vector.tensor_copy(w_dealt[:, :W_SHARE], w_walk[:, :W_SHARE, 0:2, :])
-                nc.scalar.copy(w_dealt[:, W_SHARE:], w_walk[:, W_SHARE:, 0:2, :])
+                nc.vector.tensor_copy(w_dealt[:, :W_SHARE], w_walk[:, :W_SHARE, :, 0:2])
+                nc.scalar.copy(w_dealt[:, W_SHARE:], w_walk[:, W_SHARE:, :, 0:2])
             else:
-                nc.scalar.copy(w_dealt, w_walk[:, :, 2:4, :])
+                nc.scalar.copy(w_dealt, w_walk[:, :, :, 2:4])
             if u == 1:
                 nc.vector.tensor_copy(b_picked[:], b_sb[0][:].indirect(cls_sb[:]))
             w_codes.append(keep.tile([P, 2 * P], U32, name=f"w_codes{u}", align_bytes=64))

@@ -19,6 +19,7 @@ ADD = mybir.AluOpType.add
 P = 128
 PACK = 4
 HALF = S // 2
+LINE = 2
 QUARTER = S // 4
 W_SHARE = 88
 TAIL = tuple((q * QUARTER, (q + 1) * QUARTER) for q in (0, 2, 1, 3))
@@ -67,7 +68,7 @@ def tile_picked_cbn_none_lo_kernel(tc, xT, w1, gamma, beta, offs, cls, out_0, ou
         for j in range(2):
             nc.vector.tensor_copy(x_picked[:, j, :], x_first[:, j * T : (j + 1) * T].indirect(offs_sb[:]))
         for h in range(2):
-            nc.scalar.copy(x_bf[h][:, :, 0:2], x_picked[:, :, halves[h]].rearrange("p j s -> p s j"))
+            nc.scalar.copy(x_bf[h][:, :, 0:2].rearrange("p (c i) j -> p c j i", i=LINE), x_picked[:, :, halves[h]].rearrange("p j (c i) -> p c j i", i=LINE))
         for j in range(2, PACK):
             for h in range(2):
                 nc.vector.tensor_copy(x_bf[h][:, :, j], x_late[j - 2][:].indirect(offs_sb[:, list_halves[h]]))
@@ -142,7 +143,7 @@ def tile_picked_cbn_none_lo_kernel(tc, xT, w1, gamma, beta, offs, cls, out_0, ou
                 nc.sync.dma_start(o_rows[:, t, :], row)
             if t == 1:
                 for h in range(2):
-                    nc.scalar.copy(o_bf[h][:, :, 0:2], res[0][:, :, halves[h]].rearrange("p t s -> p s t"))
+                    nc.scalar.copy(o_bf[h][:, :, 0:2].rearrange("p (c i) t -> p c t i", i=LINE), res[0][:, :, halves[h]].rearrange("p t (c i) -> p c t i", i=LINE))
 
         for t in range(PACK + 1):
             if t == 0:
@@ -157,7 +158,7 @@ def tile_picked_cbn_none_lo_kernel(tc, xT, w1, gamma, beta, offs, cls, out_0, ou
         for lo, hi in TAIL:
             h = lo // HALF
             copy = nc.vector.tensor_copy if lo == QUARTER else nc.scalar.copy
-            copy(o_bf[h][:, lo - h * HALF : hi - h * HALF, 2:4], res[1][:, :, lo:hi].rearrange("p t s -> p s t"))
+            copy(o_bf[h][:, lo - h * HALF : hi - h * HALF, 2:4].rearrange("p (c i) t -> p c t i", i=LINE), res[1][:, :, lo:hi].rearrange("p t (c i) -> p c t i", i=LINE))
         for lo, hi in TAIL[0::2] + TAIL[1::2]:
             h = lo // HALF
             nc.vector.quantize_mx(out=o_codes[:, lo:hi].bitcast(FP8X4), scales=o_scales[:, lo:hi], in_=o_bf[h][:, lo - h * HALF : hi - h * HALF, :].rearrange("p s t -> p (s t)"))

@@ -1,7 +1,6 @@
 from contextlib import ExitStack
 
 import concourse.mybir as mybir
-from concourse.masks import make_identity
 
 K, T, S, N, U = 512, 2048, 512, 512, 1024
 FLOPS = 2 * K * N * S
@@ -15,14 +14,26 @@ U8 = mybir.dt.uint8
 FP8X4 = mybir.dt.float8_e4m3fn_x4
 MULT = mybir.AluOpType.mult
 ADD = mybir.AluOpType.add
+COPY = mybir.ActivationFunctionType.Copy
 
 P = 128
 PACK = 4
 HALF = S // 2
-LINE = 2
 QUARTER = S // 4
-W_SHARE = 88
-TAIL = tuple((q * QUARTER, (q + 1) * QUARTER) for q in (0, 2, 1, 3))
+LINE = 2
+X_SHARE = 352
+
+
+def entries(lo, hi):
+    return slice(lo // 16, hi // 16)
+
+
+def woven(tile, lo, hi, first, last):
+    return tile[:, lo:hi, first:last].rearrange("p (c i) t -> p c t i", i=LINE)
+
+
+def planes(tile, lo, hi, first, last):
+    return tile[:, first:last, lo:hi].rearrange("p t (c i) -> p c t i", i=LINE)
 
 
 def tile_picked_cbn_none_lo_kernel(tc, xT, w1, gamma, beta, offs, cls, out_0, out_1, out_2):
@@ -33,137 +44,127 @@ def tile_picked_cbn_none_lo_kernel(tc, xT, w1, gamma, beta, offs, cls, out_0, ou
 
         offs_sb = keep.tile([P, S // 16], U16, name="offs_sb")
         cls_sb = keep.tile([P, S // 16], U16, name="cls_sb")
-        x_rows = xT.rearrange("(p j) c -> p j c", j=PACK)
+        x_rows = xT.rearrange("(p u j) c -> p u (j c)", u=2, j=2)
         w_rows = w1.rearrange("(p j) c -> p j c", j=PACK)
         g_rows = gamma.rearrange("(p t) c -> p t c", t=PACK)
         b_rows = beta.rearrange("(p t) c -> p t c", t=PACK)
         o_rows = out_0.rearrange("(p t) c -> p t c", t=PACK)
 
-        x_first = keep.tile([P, 2 * T], F32, name="x_first")
-        x_late = [keep.tile([P, T], F32, name=f"x{j}") for j in range(2, PACK)]
+        x_sb = [keep.tile([P, 2 * T], F32, name=f"x{u}") for u in range(2)]
         w_sb = keep.tile([P, PACK, N], F32, name="w_sb")
-        g_sb = [keep.tile([P, U], F32, name=f"g{t}") for t in range(PACK)]
+        g_pair = keep.tile([P, 2 * U], F32, name="g_pair")
+        g_sb = {t: keep.tile([P, U], F32, name=f"g{t}") for t in (2, 3)}
         b_sb = [keep.tile([P, U], F32, name=f"b{t}") for t in range(PACK)]
 
-        nc.sync.dma_start(x_first[:], x_rows[:, 0:2, :].rearrange("p j c -> p (j c)"))
+        nc.sync.dma_start(x_sb[0][:], x_rows[:, 0, :])
         nc.sync.dma_start(offs_sb[:], offs)
-        for j in range(2, PACK):
-            nc.sync.dma_start(x_late[j - 2][:], x_rows[:, j, :])
+        nc.sync.dma_start(x_sb[1][:], x_rows[:, 1, :])
         nc.sync.dma_start(cls_sb[:], cls)
         nc.sync.dma_start(w_sb[:], w_rows)
+        nc.sync.dma_start(g_pair[:], g_rows[:, 0:2, :].rearrange("p t c -> p (t c)"))
+        nc.sync.dma_start(g_sb[2][:], g_rows[:, 2, :])
         nc.sync.dma_start(b_sb[0][:], b_rows[:, 0, :])
-        nc.sync.dma_start(g_sb[0][:], g_rows[:, 0, :])
-        for t in range(1, PACK + 1):
-            if t < PACK:
-                nc.sync.dma_start(g_sb[t][:], g_rows[:, t, :])
-            if t > 1:
-                nc.sync.dma_start(b_sb[t - 1][:], b_rows[:, t - 1, :])
-        ident = keep.tile([P, P], F32, name="ident")
-        make_identity(nc, ident[:])
+        nc.sync.dma_start(b_sb[1][:], b_rows[:, 1, :])
+        nc.sync.dma_start(g_sb[3][:], g_rows[:, 3, :])
+        nc.sync.dma_start(b_sb[2][:], b_rows[:, 2, :])
+        nc.sync.dma_start(b_sb[3][:], b_rows[:, 3, :])
 
-        halves = [slice(h * HALF, (h + 1) * HALF) for h in range(2)]
-        list_halves = [slice(h * HALF // 16, (h + 1) * HALF // 16) for h in range(2)]
-        x_bf = [keep.tile([P, HALF, PACK], BF16, name=f"x_bf{h}", align_bytes=64) for h in range(2)]
-        x_picked = keep.tile([P, 2, S], F32, name="x_picked")
+        halves = ((0, HALF), (HALF, S))
+        x_picked = [keep.tile([P, 2, S], F32, name=f"x_picked{u}") for u in range(2)]
+        x_bf = keep.tile([P, S, PACK], BF16, name="x_bf", align_bytes=64)
         for j in range(2):
-            nc.vector.tensor_copy(x_picked[:, j, :], x_first[:, j * T : (j + 1) * T].indirect(offs_sb[:]))
-        for h in range(2):
-            nc.scalar.copy(x_bf[h][:, :, 0:2].rearrange("p (c i) j -> p c j i", i=LINE), x_picked[:, :, halves[h]].rearrange("p j (c i) -> p c j i", i=LINE))
-        for j in range(2, PACK):
-            for h in range(2):
-                nc.vector.tensor_copy(x_bf[h][:, :, j], x_late[j - 2][:].indirect(offs_sb[:, list_halves[h]]))
+            nc.vector.tensor_copy(x_picked[0][:, j, :], x_sb[0][:, j * T : (j + 1) * T].indirect(offs_sb[:]))
+        nc.scalar.copy(woven(x_bf, 0, S, 0, 2), planes(x_picked[0], 0, S, 0, 2))
+        for lo, hi in halves:
+            nc.scalar.activation(x_picked[1][:, 0, lo:hi], x_sb[1][:].indirect(offs_sb[:, entries(lo, hi)]), COPY)
+            nc.vector.tensor_copy(x_picked[1][:, 1, lo:hi], x_sb[1][:, T:].indirect(offs_sb[:, entries(lo, hi)]))
+        for lo, hi in ((0, HALF), (HALF, X_SHARE)):
+            nc.vector.tensor_copy(woven(x_bf, lo, hi, 2, 4), planes(x_picked[1], lo, hi, 0, 2))
+        nc.scalar.copy(woven(x_bf, X_SHARE, S, 2, 4), planes(x_picked[1], X_SHARE, S, 0, 2))
         x_codes = keep.tile([P, S], U32, name="x_codes", align_bytes=64)
         x_scales = keep.tile([P, S], U8, name="x_scales", align_bytes=64)
-        for h in range(2):
-            nc.vector.quantize_mx(out=x_codes[:, halves[h]].bitcast(FP8X4), scales=x_scales[:, halves[h]], in_=x_bf[h][:].rearrange("p s j -> p (s j)"))
+        for lo, hi in halves:
+            nc.vector.quantize_mx(out=x_codes[:, lo:hi].bitcast(FP8X4), scales=x_scales[:, lo:hi], in_=x_bf[:, lo:hi, :].rearrange("p s j -> p (s j)"))
 
         w_walk = w_sb[:].rearrange("p j (m t) -> p m j t", t=PACK)
-        b_picked = keep.tile([P, S], F32, name="b_picked")
         w_codes, w_scales = [], []
-        for u in range(2):
+        for u, copy in enumerate((nc.vector.tensor_copy, nc.scalar.copy)):
             w_bf = keep.tile([P, 2, P, PACK], BF16, name=f"w_bf{u}", align_bytes=64)
-            w_dealt = w_bf[:].rearrange("p t m j -> p m j t")
-            if u == 0:
-                nc.vector.tensor_copy(w_dealt[:, :W_SHARE], w_walk[:, :W_SHARE, :, 0:2])
-                nc.scalar.copy(w_dealt[:, W_SHARE:], w_walk[:, W_SHARE:, :, 0:2])
-            else:
-                nc.scalar.copy(w_dealt, w_walk[:, :, :, 2:4])
-            if u == 1:
-                nc.vector.tensor_copy(b_picked[:], b_sb[0][:].indirect(cls_sb[:]))
+            copy(w_bf[:].rearrange("p t m j -> p m j t"), w_walk[:, :, :, 2 * u : 2 * u + 2])
             w_codes.append(keep.tile([P, 2 * P], U32, name=f"w_codes{u}", align_bytes=64))
             w_scales.append(keep.tile([P, 2 * P], U8, name=f"w_scales{u}", align_bytes=64))
             nc.vector.quantize_mx(out=w_codes[u][:].bitcast(FP8X4), scales=w_scales[u][:], in_=w_bf[:].rearrange("p t m j -> p (t m j)"))
 
-        res = [keep.tile([P, 2, S], F32, name=f"res{u}") for u in range(2)]
-        o_bf = [keep.tile([P, HALF, PACK], BF16, name=f"o_bf{h}", align_bytes=64) for h in range(2)]
-        o_codes = keep.tile([P, S], U32, name="o_codes", align_bytes=64)
-        o_scales = keep.tile([P, S], U8, name="o_scales", align_bytes=64)
-
-        scaled = [keep.tile([P, S], F32, name=f"scaled{t}") for t in range(PACK)]
-
-
-        def scale(t, lo, hi):
-            acc = psum.tile([P, hi - lo], F32, name=f"acc{t}_{lo}")
+        acc = []
+        for t in range(PACK):
+            acc.append(psum.tile([P, S], F32, name=f"acc{t}"))
             cols = slice((t % 2) * P, (t % 2 + 1) * P)
             nc.tensor.matmul_mx(
-                out=acc[:],
+                out=acc[t][:],
                 lhsT=w_codes[t // 2][:, cols].bitcast(FP8X4),
                 lhsT_scale=w_scales[t // 2][:, cols],
-                rhs=x_codes[:, lo:hi].bitcast(FP8X4),
-                rhs_scale=x_scales[:, lo:hi],
+                rhs=x_codes[:].bitcast(FP8X4),
+                rhs_scale=x_scales[:],
                 start=True,
                 stop=True,
             )
-            y_sb = keep.tile([P, hi - lo], F32, name=f"y{t}_{lo}")
-            nc.scalar.copy(y_sb[:], acc[:])
-            nc.vector.tensor_tensor(scaled[t][:, lo:hi], g_sb[t][:].indirect(cls_sb[:, lo // 16 : hi // 16]), y_sb[:], MULT)
 
-        def shift(t):
-            row = res[t // 2][:, t % 2, :]
-            if t == 0:
-                turned = psum.tile([P, S], F32, name="turned")
-                for c in range(S // P):
-                    cols = slice(c * P, (c + 1) * P)
-                    nc.tensor.matmul(turned[:, cols], b_picked[:, cols], ident[:], start=True, stop=False, is_transpose=True)
-                    nc.tensor.matmul(turned[:, cols], scaled[t][:, cols], ident[:], start=False, stop=True, is_transpose=True)
-                turned_sb = keep.tile([P, S], F32, name="turned_sb")
-                nc.scalar.copy(turned_sb[:], turned[:])
-                back = psum.tile([P, S], F32, name="back")
-                for c in range(S // P):
-                    cols = slice(c * P, (c + 1) * P)
-                    nc.tensor.transpose(back[:, cols], turned_sb[:, cols], ident[:])
-                nc.scalar.copy(row, back[:])
-                nc.sync.dma_start(o_rows[:, t, :], row)
-            elif t < PACK - 1:
-                nc.vector.tensor_tensor(row, b_sb[t][:].indirect(cls_sb[:]), scaled[t][:], ADD)
-                nc.sync.dma_start(o_rows[:, t, :], row)
-            else:
-                for lo, hi in TAIL:
-                    nc.vector.tensor_tensor(row[:, lo:hi], b_sb[t][:].indirect(cls_sb[:, lo // 16 : hi // 16]), scaled[t][:, lo:hi], ADD)
-                nc.sync.dma_start(o_rows[:, t, :], row)
-            if t == 1:
-                for h in range(2):
-                    nc.scalar.copy(o_bf[h][:, :, 0:2].rearrange("p (c i) t -> p c t i", i=LINE), res[0][:, :, halves[h]].rearrange("p t (c i) -> p c t i", i=LINE))
+        scaled = [keep.tile([P, S], F32, name=f"scaled{t}") for t in range(PACK)]
+        res = [keep.tile([P, 2, S], F32, name=f"res{u}") for u in range(2)]
+        o_bf = keep.tile([P, S, PACK], BF16, name="o_bf", align_bytes=64)
+        o_codes = keep.tile([P, S], U32, name="o_codes", align_bytes=64)
+        o_scales = keep.tile([P, S], U8, name="o_scales", align_bytes=64)
 
-        for t in range(PACK + 1):
-            if t == 0:
-                for h in range(2):
-                    scale(t, h * HALF, (h + 1) * HALF)
-            elif t < PACK:
-                scale(t, 0, S)
-            if t > 0:
-                shift(t - 1)
+        g_picked = [keep.tile([P, S], F32, name=f"g_picked{t}", tag=f"picked{t}") for t in range(3)]
+        nc.scalar.activation(g_picked[0][:], g_pair[:].indirect(cls_sb[:]), COPY)
+        nc.vector.tensor_copy(g_picked[1][:], g_pair[:, U:].indirect(cls_sb[:]))
+        for t in range(2):
+            nc.vector.tensor_tensor(scaled[t][:], acc[t][:], g_picked[t][:], MULT)
+        for lo, hi in halves:
+            nc.scalar.activation(g_picked[2][:, lo:hi], g_sb[2][:].indirect(cls_sb[:, entries(lo, hi)]), COPY)
+            nc.vector.tensor_tensor(scaled[2][:, lo:hi], acc[2][:, lo:hi], g_picked[2][:, lo:hi], MULT)
+
+        def shift(t, lo, hi):
+            nc.vector.tensor_tensor(res[t // 2][:, t % 2, lo:hi], b_sb[t][:].indirect(cls_sb[:, entries(lo, hi)]), scaled[t][:, lo:hi], ADD)
+
+        def shift_shared(t, lo, hi):
+            b_picked = keep.tile([P, hi - lo], F32, name=f"b_picked{t}")
+            nc.scalar.activation(b_picked[:], b_sb[t][:].indirect(cls_sb[:, entries(lo, hi)]), COPY)
+            nc.vector.tensor_tensor(res[t // 2][:, t % 2, lo:hi], b_picked[:], scaled[t][:, lo:hi], ADD)
+
+        shift(0, 0, HALF)
+        shift_shared(0, HALF, S)
+        nc.sync.dma_start(o_rows[:, 0, :], res[0][:, 0, :])
+        y_last = keep.tile([P, S], F32, name="y_last", tag="picked2")
+        nc.scalar.copy(y_last[:], acc[3][:])
+        shift(1, 0, HALF)
+        shift_shared(1, HALF, S)
+        nc.sync.dma_start(o_rows[:, 1, :], res[0][:, 1, :])
+        nc.scalar.copy(woven(o_bf, 0, S, 0, 2), planes(res[0], 0, S, 0, 2))
+        nc.vector.tensor_tensor(scaled[3][:], g_sb[3][:].indirect(cls_sb[:]), y_last[:], MULT)
+        shift(2, 0, S)
+        nc.sync.dma_start(o_rows[:, 2, :], res[1][:, 0, :])
+
+        quarters = [(q * QUARTER, (q + 1) * QUARTER) for q in range(4)]
+        for lo, hi in quarters[:3]:
+            shift(3, lo, hi)
+        shift_shared(3, *quarters[3])
+        nc.sync.dma_start(o_rows[:, 3, :], res[1][:, 1, :])
+        for lo, hi in quarters[:3]:
+            nc.scalar.copy(woven(o_bf, lo, hi, 2, 4), planes(res[1], lo, hi, 0, 2))
 
         words = out_1.rearrange("z p s r -> p (z s r)").bitcast(I32)
-        for lo, hi in TAIL:
-            h = lo // HALF
-            copy = nc.vector.tensor_copy if lo == QUARTER else nc.scalar.copy
-            copy(o_bf[h][:, lo - h * HALF : hi - h * HALF, 2:4].rearrange("p (c i) t -> p c t i", i=LINE), res[1][:, :, lo:hi].rearrange("p t (c i) -> p c t i", i=LINE))
-        for lo, hi in TAIL[0::2] + TAIL[1::2]:
-            h = lo // HALF
-            nc.vector.quantize_mx(out=o_codes[:, lo:hi].bitcast(FP8X4), scales=o_scales[:, lo:hi], in_=o_bf[h][:, lo - h * HALF : hi - h * HALF, :].rearrange("p s t -> p (s t)"))
-            if hi % HALF == 0:
-                nc.sync.dma_start(words[:, hi - HALF : hi], o_codes[:, hi - HALF : hi].bitcast(I32))
+
+        def quantise(lo, hi):
+            nc.vector.quantize_mx(out=o_codes[:, lo:hi].bitcast(FP8X4), scales=o_scales[:, lo:hi], in_=o_bf[:, lo:hi, :].rearrange("p s t -> p (s t)"))
+
+        quantise(*quarters[0])
+        nc.vector.tensor_copy(woven(o_bf, *quarters[3], 2, 4), planes(res[1], *quarters[3], 0, 2))
+        quantise(*quarters[1])
+        nc.sync.dma_start(words[:, :HALF], o_codes[:, :HALF].bitcast(I32))
+        quantise(*quarters[3])
+        quantise(*quarters[2])
+        nc.sync.dma_start(words[:, HALF:], o_codes[:, HALF:].bitcast(I32))
         scale_rows = out_2.rearrange("z q s -> (z q) s").bitcast(I32)
         for q in range(4):
             queue = nc.scalar if q % 2 == 0 else nc.sync

@@ -110,7 +110,7 @@ def tile_picked_cbn_none_lo_kernel(tc, xT, w1, gamma, beta, offs, cls, out_0, ou
             )
 
         scaled = [keep.tile([P, S], F32, name=f"scaled{t}") for t in range(PACK)]
-        res = [keep.tile([P, 2, S], F32, name=f"res{u}") for u in range(2)]
+        res = keep.tile([P, PACK, S], F32, name="res")
         o_bf = keep.tile([P, S, PACK], BF16, name="o_bf", align_bytes=64)
         o_codes = keep.tile([P, S], U32, name="o_codes", align_bytes=64)
         o_scales = keep.tile([P, S], U8, name="o_scales", align_bytes=64)
@@ -125,33 +125,32 @@ def tile_picked_cbn_none_lo_kernel(tc, xT, w1, gamma, beta, offs, cls, out_0, ou
             nc.vector.tensor_tensor(scaled[2][:, lo:hi], acc[2][:, lo:hi], g_picked[2][:, lo:hi], MULT)
 
         def shift(t, lo, hi):
-            nc.vector.tensor_tensor(res[t // 2][:, t % 2, lo:hi], b_sb[t][:].indirect(cls_sb[:, entries(lo, hi)]), scaled[t][:, lo:hi], ADD)
+            nc.vector.tensor_tensor(res[:, t, lo:hi], b_sb[t][:].indirect(cls_sb[:, entries(lo, hi)]), scaled[t][:, lo:hi], ADD)
 
         def shift_shared(t, lo, hi):
             b_picked = keep.tile([P, hi - lo], F32, name=f"b_picked{t}")
             nc.scalar.activation(b_picked[:], b_sb[t][:].indirect(cls_sb[:, entries(lo, hi)]), COPY)
-            nc.vector.tensor_tensor(res[t // 2][:, t % 2, lo:hi], b_picked[:], scaled[t][:, lo:hi], ADD)
+            nc.vector.tensor_tensor(res[:, t, lo:hi], b_picked[:], scaled[t][:, lo:hi], ADD)
 
         shift(0, 0, HALF)
         shift_shared(0, HALF, S)
-        nc.sync.dma_start(o_rows[:, 0, :], res[0][:, 0, :])
+        nc.sync.dma_start(o_rows[:, 0, :], res[:, 0, :])
         y_last = keep.tile([P, S], F32, name="y_last", tag="picked2")
         nc.scalar.copy(y_last[:], acc[3][:])
         shift(1, 0, HALF)
         shift_shared(1, HALF, S)
-        nc.sync.dma_start(o_rows[:, 1, :], res[0][:, 1, :])
-        nc.scalar.copy(woven(o_bf, 0, S, 0, 2), planes(res[0], 0, S, 0, 2))
+        nc.sync.dma_start(o_rows[:, 1, :], res[:, 1, :])
         nc.vector.tensor_tensor(scaled[3][:], g_sb[3][:].indirect(cls_sb[:]), y_last[:], MULT)
         shift(2, 0, S)
-        nc.sync.dma_start(o_rows[:, 2, :], res[1][:, 0, :])
+        nc.sync.dma_start(o_rows[:, 2, :], res[:, 2, :])
 
         quarters = [(q * QUARTER, (q + 1) * QUARTER) for q in range(4)]
         for lo, hi in quarters[:3]:
             shift(3, lo, hi)
         shift_shared(3, *quarters[3])
-        nc.sync.dma_start(o_rows[:, 3, :], res[1][:, 1, :])
+        nc.sync.dma_start(o_rows[:, 3, :], res[:, 3, :])
         for lo, hi in quarters[:3]:
-            nc.scalar.copy(woven(o_bf, lo, hi, 2, 4), planes(res[1], lo, hi, 0, 2))
+            nc.scalar.copy(woven(o_bf, lo, hi, 0, PACK), planes(res, lo, hi, 0, PACK))
 
         words = out_1.rearrange("z p s r -> p (z s r)").bitcast(I32)
 
@@ -159,7 +158,7 @@ def tile_picked_cbn_none_lo_kernel(tc, xT, w1, gamma, beta, offs, cls, out_0, ou
             nc.vector.quantize_mx(out=o_codes[:, lo:hi].bitcast(FP8X4), scales=o_scales[:, lo:hi], in_=o_bf[:, lo:hi, :].rearrange("p s t -> p (s t)"))
 
         quantise(*quarters[0])
-        nc.vector.tensor_copy(woven(o_bf, *quarters[3], 2, 4), planes(res[1], *quarters[3], 0, 2))
+        nc.vector.tensor_copy(woven(o_bf, *quarters[3], 0, PACK), planes(res, *quarters[3], 0, PACK))
         quantise(*quarters[1])
         nc.sync.dma_start(words[:, :HALF], o_codes[:, :HALF].bitcast(I32))
         quantise(*quarters[3])

@@ -22,6 +22,7 @@ HALF = S // 2
 QUARTER = S // 4
 LINE = 2
 X_SHARE = 352
+O_SHARE = 320
 
 
 def entries(lo, hi):
@@ -117,9 +118,11 @@ def tile_picked_cbn_none_lo_kernel(tc, xT, w1, gamma, beta, offs, cls, out_0, ou
 
         g_picked = [keep.tile([P, S], F32, name=f"g_picked{t}", tag=f"picked{t}") for t in range(3)]
         nc.scalar.activation(g_picked[0][:], g_pair[:].indirect(cls_sb[:]), COPY)
-        nc.vector.tensor_copy(g_picked[1][:], g_pair[:, U:].indirect(cls_sb[:]))
-        for t in range(2):
-            nc.vector.tensor_tensor(scaled[t][:], acc[t][:], g_picked[t][:], MULT)
+        for lo, hi in halves:
+            nc.vector.tensor_copy(g_picked[1][:, lo:hi], g_pair[:, U:].indirect(cls_sb[:, entries(lo, hi)]))
+        for lo, hi in halves:
+            nc.vector.tensor_tensor(scaled[1][:, lo:hi], acc[1][:, lo:hi], g_picked[1][:, lo:hi], MULT)
+        nc.vector.tensor_tensor(scaled[0][:], acc[0][:], g_picked[0][:], MULT)
         for lo, hi in halves:
             nc.scalar.activation(g_picked[2][:, lo:hi], g_sb[2][:].indirect(cls_sb[:, entries(lo, hi)]), COPY)
             nc.vector.tensor_tensor(scaled[2][:, lo:hi], acc[2][:, lo:hi], g_picked[2][:, lo:hi], MULT)
@@ -135,13 +138,17 @@ def tile_picked_cbn_none_lo_kernel(tc, xT, w1, gamma, beta, offs, cls, out_0, ou
         shift(0, 0, HALF)
         shift_shared(0, HALF, S)
         nc.sync.dma_start(o_rows[:, 0, :], res[:, 0, :])
-        y_last = keep.tile([P, S], F32, name="y_last", tag="picked2")
-        nc.scalar.copy(y_last[:], acc[3][:])
+        y_last = keep.tile([P, HALF], F32, name="y_last", tag="picked2")
+        nc.scalar.copy(y_last[:], acc[3][:, :HALF])
         shift(1, 0, HALF)
         shift_shared(1, HALF, S)
         nc.sync.dma_start(o_rows[:, 1, :], res[:, 1, :])
-        nc.vector.tensor_tensor(scaled[3][:], g_sb[3][:].indirect(cls_sb[:]), y_last[:], MULT)
-        shift(2, 0, S)
+        nc.vector.tensor_tensor(scaled[3][:, :HALF], g_sb[3][:].indirect(cls_sb[:, entries(0, HALF)]), y_last[:], MULT)
+        g_last = keep.tile([P, HALF], F32, name="g_last")
+        nc.scalar.activation(g_last[:], g_sb[3][:].indirect(cls_sb[:, entries(HALF, S)]), COPY)
+        nc.vector.tensor_tensor(scaled[3][:, HALF:], acc[3][:, HALF:], g_last[:], MULT)
+        shift(2, 0, HALF)
+        shift_shared(2, HALF, S)
         nc.sync.dma_start(o_rows[:, 2, :], res[:, 2, :])
 
         quarters = [(q * QUARTER, (q + 1) * QUARTER) for q in range(4)]
@@ -149,7 +156,7 @@ def tile_picked_cbn_none_lo_kernel(tc, xT, w1, gamma, beta, offs, cls, out_0, ou
             shift(3, lo, hi)
         shift_shared(3, *quarters[3])
         nc.sync.dma_start(o_rows[:, 3, :], res[:, 3, :])
-        for lo, hi in quarters[:3]:
+        for lo, hi in quarters[:2] + [(HALF, O_SHARE)]:
             nc.scalar.copy(woven(o_bf, lo, hi, 0, PACK), planes(res, lo, hi, 0, PACK))
 
         words = out_1.rearrange("z p s r -> p (z s r)").bitcast(I32)
@@ -158,11 +165,10 @@ def tile_picked_cbn_none_lo_kernel(tc, xT, w1, gamma, beta, offs, cls, out_0, ou
             nc.vector.quantize_mx(out=o_codes[:, lo:hi].bitcast(FP8X4), scales=o_scales[:, lo:hi], in_=o_bf[:, lo:hi, :].rearrange("p s t -> p (s t)"))
 
         quantise(*quarters[0])
-        nc.vector.tensor_copy(woven(o_bf, *quarters[3], 0, PACK), planes(res, *quarters[3], 0, PACK))
+        nc.vector.tensor_copy(woven(o_bf, O_SHARE, S, 0, PACK), planes(res, O_SHARE, S, 0, PACK))
         quantise(*quarters[1])
         nc.sync.dma_start(words[:, :HALF], o_codes[:, :HALF].bitcast(I32))
-        quantise(*quarters[3])
-        quantise(*quarters[2])
+        quantise(HALF, S)
         nc.sync.dma_start(words[:, HALF:], o_codes[:, HALF:].bitcast(I32))
         scale_rows = out_2.rearrange("z q s -> (z q) s").bitcast(I32)
         for q in range(4):

@@ -22,7 +22,7 @@ HALF = S // 2
 QUARTER = S // 4
 LINE = 2
 X_SHARE = 352
-O_SHARE = 320
+FUSED = 192
 
 
 def entries(lo, hi):
@@ -131,45 +131,40 @@ def tile_picked_cbn_none_lo_kernel(tc, xT, w1, gamma, beta, offs, cls, out_0, ou
             nc.vector.tensor_tensor(res[:, t, lo:hi], b_sb[t][:].indirect(cls_sb[:, entries(lo, hi)]), scaled[t][:, lo:hi], ADD)
 
         def shift_shared(t, lo, hi):
-            b_picked = keep.tile([P, hi - lo], F32, name=f"b_picked{t}")
+            b_picked = keep.tile([P, hi - lo], F32, name=f"b_picked{t}_{lo}")
             nc.scalar.activation(b_picked[:], b_sb[t][:].indirect(cls_sb[:, entries(lo, hi)]), COPY)
             nc.vector.tensor_tensor(res[:, t, lo:hi], b_picked[:], scaled[t][:, lo:hi], ADD)
 
         shift(0, 0, HALF)
         shift_shared(0, HALF, S)
         nc.sync.dma_start(o_rows[:, 0, :], res[:, 0, :])
-        y_last = keep.tile([P, HALF], F32, name="y_last", tag="picked2")
-        nc.scalar.copy(y_last[:], acc[3][:, :HALF])
-        shift(1, 0, HALF)
-        shift_shared(1, HALF, S)
+        y_last = keep.tile([P, FUSED], F32, name="y_last", tag="picked0")
+        nc.scalar.copy(y_last[:], acc[3][:, :FUSED])
+        shift(1, 0, FUSED)
+        shift_shared(1, FUSED, S)
         nc.sync.dma_start(o_rows[:, 1, :], res[:, 1, :])
-        nc.vector.tensor_tensor(scaled[3][:, :HALF], g_sb[3][:].indirect(cls_sb[:, entries(0, HALF)]), y_last[:], MULT)
-        g_last = keep.tile([P, HALF], F32, name="g_last")
-        nc.scalar.activation(g_last[:], g_sb[3][:].indirect(cls_sb[:, entries(HALF, S)]), COPY)
-        nc.vector.tensor_tensor(scaled[3][:, HALF:], acc[3][:, HALF:], g_last[:], MULT)
+        nc.vector.tensor_tensor(scaled[3][:, :FUSED], g_sb[3][:].indirect(cls_sb[:, entries(0, FUSED)]), y_last[:], MULT)
+        g_last = keep.tile([P, S - FUSED], F32, name="g_last")
+        nc.scalar.activation(g_last[:], g_sb[3][:].indirect(cls_sb[:, entries(FUSED, S)]), COPY)
+        nc.vector.tensor_tensor(scaled[3][:, FUSED:], acc[3][:, FUSED:], g_last[:], MULT)
         shift(2, 0, HALF)
         shift_shared(2, HALF, S)
         nc.sync.dma_start(o_rows[:, 2, :], res[:, 2, :])
 
-        quarters = [(q * QUARTER, (q + 1) * QUARTER) for q in range(4)]
-        for lo, hi in quarters[:3]:
-            shift(3, lo, hi)
-        shift_shared(3, *quarters[3])
+        pieces = tuple((q * QUARTER, (q + 1) * QUARTER) for q in range(4))
+        for q in range(2):
+            shift(3, *pieces[q])
+            shift_shared(3, *pieces[q + 2])
         nc.sync.dma_start(o_rows[:, 3, :], res[:, 3, :])
-        for lo, hi in quarters[:2] + [(HALF, O_SHARE)]:
-            nc.scalar.copy(woven(o_bf, lo, hi, 0, PACK), planes(res, lo, hi, 0, PACK))
+        for q in range(2):
+            nc.scalar.copy(woven(o_bf, *pieces[q], 0, PACK), planes(res, *pieces[q], 0, PACK))
+            nc.vector.tensor_copy(woven(o_bf, *pieces[q + 2], 0, PACK), planes(res, *pieces[q + 2], 0, PACK))
 
         words = out_1.rearrange("z p s r -> p (z s r)").bitcast(I32)
-
-        def quantise(lo, hi):
+        for lo, hi in ((0, QUARTER), (QUARTER, HALF), (HALF, S)):
             nc.vector.quantize_mx(out=o_codes[:, lo:hi].bitcast(FP8X4), scales=o_scales[:, lo:hi], in_=o_bf[:, lo:hi, :].rearrange("p s t -> p (s t)"))
-
-        quantise(*quarters[0])
-        nc.vector.tensor_copy(woven(o_bf, O_SHARE, S, 0, PACK), planes(res, O_SHARE, S, 0, PACK))
-        quantise(*quarters[1])
-        nc.sync.dma_start(words[:, :HALF], o_codes[:, :HALF].bitcast(I32))
-        quantise(HALF, S)
-        nc.sync.dma_start(words[:, HALF:], o_codes[:, HALF:].bitcast(I32))
+            if hi % HALF == 0:
+                nc.sync.dma_start(words[:, hi - HALF : hi], o_codes[:, hi - HALF : hi].bitcast(I32))
         scale_rows = out_2.rearrange("z q s -> (z q) s").bitcast(I32)
         for q in range(4):
             queue = nc.scalar if q % 2 == 0 else nc.sync

@@ -20,7 +20,6 @@ P = 128
 PACK = 4
 HALF = S // 2
 QUARTER = S // 4
-LINE = 2
 X_SHARE = 352
 FUSED = 192
 
@@ -30,11 +29,11 @@ def entries(lo, hi):
 
 
 def woven(tile, lo, hi, first, last):
-    return tile[:, lo:hi, first:last].rearrange("p (c i) t -> p c t i", i=LINE)
+    return tile[:, lo:hi, first:last].rearrange("p (c i) t -> p c t i", i=last - first)
 
 
 def planes(tile, lo, hi, first, last):
-    return tile[:, first:last, lo:hi].rearrange("p t (c i) -> p c t i", i=LINE)
+    return tile[:, first:last, lo:hi].rearrange("p t (c i) -> p c t i", i=last - first)
 
 
 def tile_picked_cbn_none_lo_kernel(tc, xT, w1, gamma, beta, offs, cls, out_0, out_1, out_2):

@@ -136,12 +136,11 @@ def tile_picked_cbn_none_lo_kernel(tc, xT, w1, gamma, beta, offs, cls, out_0, ou
 
         shift(0, 0, HALF)
         shift_shared(0, HALF, S)
-        nc.sync.dma_start(o_rows[:, 0, :], res[:, 0, :])
         y_last = keep.tile([P, FUSED], F32, name="y_last", tag="picked0")
         nc.scalar.copy(y_last[:], acc[3][:, :FUSED])
         shift(1, 0, FUSED)
         shift_shared(1, FUSED, S)
-        nc.sync.dma_start(o_rows[:, 1, :], res[:, 1, :])
+        nc.sync.dma_start(o_rows[:, 0:2, :], res[:, 0:2, :])
         nc.vector.tensor_tensor(scaled[3][:, :FUSED], g_sb[3][:].indirect(cls_sb[:, entries(0, FUSED)]), y_last[:], MULT)
         g_last = keep.tile([P, S - FUSED], F32, name="g_last")
         nc.scalar.activation(g_last[:], g_sb[3][:].indirect(cls_sb[:, entries(FUSED, S)]), COPY)
@@ -160,10 +159,9 @@ def tile_picked_cbn_none_lo_kernel(tc, xT, w1, gamma, beta, offs, cls, out_0, ou
             nc.vector.tensor_copy(woven(o_bf, *pieces[q + 2], 0, PACK), planes(res, *pieces[q + 2], 0, PACK))
 
         words = out_1.rearrange("z p s r -> p (z s r)").bitcast(I32)
-        for lo, hi in ((0, QUARTER), (QUARTER, HALF), (HALF, S)):
+        for lo, hi in (pieces[0], (HALF, S), pieces[1]):
             nc.vector.quantize_mx(out=o_codes[:, lo:hi].bitcast(FP8X4), scales=o_scales[:, lo:hi], in_=o_bf[:, lo:hi, :].rearrange("p s t -> p (s t)"))
-            if hi % HALF == 0:
-                nc.sync.dma_start(words[:, hi - HALF : hi], o_codes[:, hi - HALF : hi].bitcast(I32))
+            nc.sync.dma_start(words[:, lo:hi], o_codes[:, lo:hi].bitcast(I32))
         scale_rows = out_2.rearrange("z q s -> (z q) s").bitcast(I32)
         for q in range(4):
             queue = nc.scalar if q % 2 == 0 else nc.sync

@@ -22,6 +22,7 @@ HALF = S // 2
 QUARTER = S // 4
 X_SHARE = 352
 FUSED = 192
+TAIL_FUSED = 320
 
 
 def entries(lo, hi):
@@ -74,7 +75,8 @@ def tile_picked_cbn_none_lo_kernel(tc, xT, w1, gamma, beta, offs, cls, out_0, ou
         x_bf = keep.tile([P, S, PACK], BF16, name="x_bf", align_bytes=64)
         for j in range(2):
             nc.vector.tensor_copy(x_picked[0][:, j, :], x_sb[0][:, j * T : (j + 1) * T].indirect(offs_sb[:]))
-        nc.scalar.copy(woven(x_bf, 0, S, 0, 2), planes(x_picked[0], 0, S, 0, 2))
+        for lo, hi in halves:
+            nc.scalar.copy(woven(x_bf, lo, hi, 0, 2), planes(x_picked[0], lo, hi, 0, 2))
         for lo, hi in halves:
             nc.scalar.activation(x_picked[1][:, 0, lo:hi], x_sb[1][:].indirect(offs_sb[:, entries(lo, hi)]), COPY)
             nc.vector.tensor_copy(x_picked[1][:, 1, lo:hi], x_sb[1][:, T:].indirect(offs_sb[:, entries(lo, hi)]))
@@ -150,18 +152,22 @@ def tile_picked_cbn_none_lo_kernel(tc, xT, w1, gamma, beta, offs, cls, out_0, ou
         nc.sync.dma_start(o_rows[:, 2, :], res[:, 2, :])
 
         pieces = tuple((q * QUARTER, (q + 1) * QUARTER) for q in range(4))
-        for q in range(2):
-            shift(3, *pieces[q])
-            shift_shared(3, *pieces[q + 2])
+        shift(3, *pieces[0])
+        shift(3, QUARTER, TAIL_FUSED)
+        shift_shared(3, TAIL_FUSED, S)
         nc.sync.dma_start(o_rows[:, 3, :], res[:, 3, :])
-        for q in range(2):
-            nc.scalar.copy(woven(o_bf, *pieces[q], 0, PACK), planes(res, *pieces[q], 0, PACK))
-            nc.vector.tensor_copy(woven(o_bf, *pieces[q + 2], 0, PACK), planes(res, *pieces[q + 2], 0, PACK))
+        for lo, hi in (pieces[0], pieces[3]):
+            nc.scalar.copy(woven(o_bf, lo, hi, 0, PACK), planes(res, lo, hi, 0, PACK))
+        for lo, hi in ((QUARTER, TAIL_FUSED), (TAIL_FUSED, 3 * QUARTER)):
+            nc.vector.tensor_copy(woven(o_bf, lo, hi, 0, PACK), planes(res, lo, hi, 0, PACK))
 
         words = out_1.rearrange("z p s r -> p (z s r)").bitcast(I32)
-        for lo, hi in (pieces[0], (HALF, S), pieces[1]):
+        stored = 0
+        for lo, hi in pieces:
             nc.vector.quantize_mx(out=o_codes[:, lo:hi].bitcast(FP8X4), scales=o_scales[:, lo:hi], in_=o_bf[:, lo:hi, :].rearrange("p s t -> p (s t)"))
-            nc.sync.dma_start(words[:, lo:hi], o_codes[:, lo:hi].bitcast(I32))
+            if hi >= HALF:
+                nc.sync.dma_start(words[:, stored:hi], o_codes[:, stored:hi].bitcast(I32))
+                stored = hi
         scale_rows = out_2.rearrange("z q s -> (z q) s").bitcast(I32)
         for q in range(4):
             queue = nc.scalar if q % 2 == 0 else nc.sync

@@ -170,5 +170,5 @@ def tile_picked_cbn_none_lo_kernel(tc, xT, w1, gamma, beta, offs, cls, out_0, ou
                 stored = hi
         scale_rows = out_2.rearrange("z q s -> (z q) s").bitcast(I32)
         for q in range(4):
-            queue = nc.scalar if q % 2 == 0 else nc.sync
+            queue = nc.scalar if q < 2 else nc.sync
             queue.dma_start(scale_rows[4 * q : 4 * q + 4, :], o_scales[32 * q : 32 * q + 4, :].bitcast(I32))

from contextlib import ExitStack

import concourse.mybir as mybir

K, T, S, N, U = 512, 2048, 512, 512, 1024
FLOPS = 2 * K * N * S

F32 = mybir.dt.float32
BF16 = mybir.dt.bfloat16
I32 = mybir.dt.int32
U32 = mybir.dt.uint32
U16 = mybir.dt.uint16
U8 = mybir.dt.uint8
FP8X4 = mybir.dt.float8_e4m3fn_x4
MULT = mybir.AluOpType.mult
ADD = mybir.AluOpType.add
COPY = mybir.ActivationFunctionType.Copy

P = 128
PACK = 4
HALF = S // 2
QUARTER = S // 4
X_SHARE = 352
FUSED = 192
TAIL_FUSED = 320


def entries(lo, hi):
    return slice(lo // 16, hi // 16)


def woven(tile, lo, hi, first, last):
    return tile[:, lo:hi, first:last].rearrange("p (c i) t -> p c t i", i=last - first)


def planes(tile, lo, hi, first, last):
    return tile[:, first:last, lo:hi].rearrange("p t (c i) -> p c t i", i=last - first)


def tile_picked_cbn_none_lo_kernel(tc, xT, w1, gamma, beta, offs, cls, out_0, out_1, out_2):
    nc = tc.nc
    with ExitStack() as ctx:
        keep = ctx.enter_context(tc.tile_pool(name="keep", bufs=1))
        psum = ctx.enter_context(tc.psum_pool(name="psum", bufs=1))

        offs_sb = keep.tile([P, S // 16], U16, name="offs_sb")
        cls_sb = keep.tile([P, S // 16], U16, name="cls_sb")
        x_rows = xT.rearrange("(p u j) c -> p u (j c)", u=2, j=2)
        w_rows = w1.rearrange("(p j) c -> p j c", j=PACK)
        g_rows = gamma.rearrange("(p t) c -> p t c", t=PACK)
        b_rows = beta.rearrange("(p t) c -> p t c", t=PACK)
        o_rows = out_0.rearrange("(p t) c -> p t c", t=PACK)

        x_sb = [keep.tile([P, 2 * T], F32, name=f"x{u}") for u in range(2)]
        w_sb = keep.tile([P, PACK, N], F32, name="w_sb")
        g_pair = keep.tile([P, 2 * U], F32, name="g_pair")
        g_sb = {t: keep.tile([P, U], F32, name=f"g{t}") for t in (2, 3)}
        b_sb = [keep.tile([P, U], F32, name=f"b{t}") for t in range(PACK)]

        nc.sync.dma_start(x_sb[0][:], x_rows[:, 0, :])
        nc.sync.dma_start(offs_sb[:], offs)
        nc.sync.dma_start(x_sb[1][:], x_rows[:, 1, :])
        nc.sync.dma_start(cls_sb[:], cls)
        nc.sync.dma_start(w_sb[:], w_rows)
        nc.sync.dma_start(g_pair[:], g_rows[:, 0:2, :].rearrange("p t c -> p (t c)"))
        nc.sync.dma_start(g_sb[2][:], g_rows[:, 2, :])
        nc.sync.dma_start(b_sb[0][:], b_rows[:, 0, :])
        nc.sync.dma_start(b_sb[1][:], b_rows[:, 1, :])
        nc.sync.dma_start(g_sb[3][:], g_rows[:, 3, :])
        nc.sync.dma_start(b_sb[2][:], b_rows[:, 2, :])
        nc.sync.dma_start(b_sb[3][:], b_rows[:, 3, :])

        halves = ((0, HALF), (HALF, S))
        x_picked = [keep.tile([P, 2, S], F32, name=f"x_picked{u}") for u in range(2)]
        x_bf = keep.tile([P, S, PACK], BF16, name="x_bf", align_bytes=64)
        for j in range(2):
            nc.vector.tensor_copy(x_picked[0][:, j, :], x_sb[0][:, j * T : (j + 1) * T].indirect(offs_sb[:]))
        for lo, hi in halves:
            nc.scalar.copy(woven(x_bf, lo, hi, 0, 2), planes(x_picked[0], lo, hi, 0, 2))
        for lo, hi in halves:
            nc.scalar.activation(x_picked[1][:, 0, lo:hi], x_sb[1][:].indirect(offs_sb[:, entries(lo, hi)]), COPY)
            nc.vector.tensor_copy(x_picked[1][:, 1, lo:hi], x_sb[1][:, T:].indirect(offs_sb[:, entries(lo, hi)]))
        for lo, hi in ((0, HALF), (HALF, X_SHARE)):
            nc.vector.tensor_copy(woven(x_bf, lo, hi, 2, 4), planes(x_picked[1], lo, hi, 0, 2))
        nc.scalar.copy(woven(x_bf, X_SHARE, S, 2, 4), planes(x_picked[1], X_SHARE, S, 0, 2))
        x_codes = keep.tile([P, S], U32, name="x_codes", align_bytes=64)
        x_scales = keep.tile([P, S], U8, name="x_scales", align_bytes=64)
        for lo, hi in halves:
            nc.vector.quantize_mx(out=x_codes[:, lo:hi].bitcast(FP8X4), scales=x_scales[:, lo:hi], in_=x_bf[:, lo:hi, :].rearrange("p s j -> p (s j)"))

        w_walk = w_sb[:].rearrange("p j (m t) -> p m j t", t=PACK)
        w_codes, w_scales = [], []
        for u, copy in enumerate((nc.vector.tensor_copy, nc.scalar.copy)):
            w_bf = keep.tile([P, 2, P, PACK], BF16, name=f"w_bf{u}", align_bytes=64)
            copy(w_bf[:].rearrange("p t m j -> p m j t"), w_walk[:, :, :, 2 * u : 2 * u + 2])
            w_codes.append(keep.tile([P, 2 * P], U32, name=f"w_codes{u}", align_bytes=64))
            w_scales.append(keep.tile([P, 2 * P], U8, name=f"w_scales{u}", align_bytes=64))
            nc.vector.quantize_mx(out=w_codes[u][:].bitcast(FP8X4), scales=w_scales[u][:], in_=w_bf[:].rearrange("p t m j -> p (t m j)"))

        acc = []
        for t in range(PACK):
            acc.append(psum.tile([P, S], F32, name=f"acc{t}"))
            cols = slice((t % 2) * P, (t % 2 + 1) * P)
            nc.tensor.matmul_mx(
                out=acc[t][:],
                lhsT=w_codes[t // 2][:, cols].bitcast(FP8X4),
                lhsT_scale=w_scales[t // 2][:, cols],
                rhs=x_codes[:].bitcast(FP8X4),
                rhs_scale=x_scales[:],
                start=True,
                stop=True,
            )

        scaled = [keep.tile([P, S], F32, name=f"scaled{t}") for t in range(PACK)]
        res = keep.tile([P, PACK, S], F32, name="res")
        o_bf = keep.tile([P, S, PACK], BF16, name="o_bf", align_bytes=64)
        o_codes = keep.tile([P, S], U32, name="o_codes", align_bytes=64)
        o_scales = keep.tile([P, S], U8, name="o_scales", align_bytes=64)

        g_picked = [keep.tile([P, S], F32, name=f"g_picked{t}", tag=f"picked{t}") for t in range(3)]
        nc.scalar.activation(g_picked[0][:], g_pair[:].indirect(cls_sb[:]), COPY)
        for lo, hi in halves:
            nc.vector.tensor_copy(g_picked[1][:, lo:hi], g_pair[:, U:].indirect(cls_sb[:, entries(lo, hi)]))
        for lo, hi in halves:
            nc.vector.tensor_tensor(scaled[1][:, lo:hi], acc[1][:, lo:hi], g_picked[1][:, lo:hi], MULT)
        nc.vector.tensor_tensor(scaled[0][:], acc[0][:], g_picked[0][:], MULT)
        for lo, hi in halves:
            nc.scalar.activation(g_picked[2][:, lo:hi], g_sb[2][:].indirect(cls_sb[:, entries(lo, hi)]), COPY)
            nc.vector.tensor_tensor(scaled[2][:, lo:hi], acc[2][:, lo:hi], g_picked[2][:, lo:hi], MULT)

        def shift(t, lo, hi):
            nc.vector.tensor_tensor(res[:, t, lo:hi], b_sb[t][:].indirect(cls_sb[:, entries(lo, hi)]), scaled[t][:, lo:hi], ADD)

        def shift_shared(t, lo, hi):
            b_picked = keep.tile([P, hi - lo], F32, name=f"b_picked{t}_{lo}")
            nc.scalar.activation(b_picked[:], b_sb[t][:].indirect(cls_sb[:, entries(lo, hi)]), COPY)
            nc.vector.tensor_tensor(res[:, t, lo:hi], b_picked[:], scaled[t][:, lo:hi], ADD)

        shift(0, 0, HALF)
        shift_shared(0, HALF, S)
        y_last = keep.tile([P, FUSED], F32, name="y_last", tag="picked0")
        nc.scalar.copy(y_last[:], acc[3][:, :FUSED])
        shift(1, 0, FUSED)
        shift_shared(1, FUSED, S)
        nc.sync.dma_start(o_rows[:, 0:2, :], res[:, 0:2, :])
        nc.vector.tensor_tensor(scaled[3][:, :FUSED], g_sb[3][:].indirect(cls_sb[:, entries(0, FUSED)]), y_last[:], MULT)
        g_last = keep.tile([P, S - FUSED], F32, name="g_last")
        nc.scalar.activation(g_last[:], g_sb[3][:].indirect(cls_sb[:, entries(FUSED, S)]), COPY)
        nc.vector.tensor_tensor(scaled[3][:, FUSED:], acc[3][:, FUSED:], g_last[:], MULT)
        shift(2, 0, HALF)
        shift_shared(2, HALF, S)
        nc.sync.dma_start(o_rows[:, 2, :], res[:, 2, :])

        pieces = tuple((q * QUARTER, (q + 1) * QUARTER) for q in range(4))
        shift(3, *pieces[0])
        shift(3, QUARTER, TAIL_FUSED)
        shift_shared(3, TAIL_FUSED, S)
        nc.sync.dma_start(o_rows[:, 3, :], res[:, 3, :])
        for lo, hi in (pieces[0], pieces[3]):
            nc.scalar.copy(woven(o_bf, lo, hi, 0, PACK), planes(res, lo, hi, 0, PACK))
        for lo, hi in ((QUARTER, TAIL_FUSED), (TAIL_FUSED, 3 * QUARTER)):
            nc.vector.tensor_copy(woven(o_bf, lo, hi, 0, PACK), planes(res, lo, hi, 0, PACK))

        words = out_1.rearrange("z p s r -> p (z s r)").bitcast(I32)
        stored = 0
        for lo, hi in pieces:
            nc.vector.quantize_mx(out=o_codes[:, lo:hi].bitcast(FP8X4), scales=o_scales[:, lo:hi], in_=o_bf[:, lo:hi, :].rearrange("p s t -> p (s t)"))
            if hi >= HALF:
                nc.sync.dma_start(words[:, stored:hi], o_codes[:, stored:hi].bitcast(I32))
                stored = hi
        scale_rows = out_2.rearrange("z q s -> (z q) s").bitcast(I32)
        for q in range(4):
            queue = nc.scalar if q < 2 else nc.sync
            queue.dma_start(scale_rows[4 * q : 4 * q + 4, :], o_scales[32 * q : 32 * q + 4, :].bitcast(I32))
